import numpy as np
import ml_dtypes


def mxq(x, axis, fmt="e4m3"):
    dtype, down = {"e4m3": (ml_dtypes.float8_e4m3fn, 7), "e5m2": (ml_dtypes.float8_e5m2, 14)}[fmt]
    v = np.moveaxis(np.asarray(x, np.float32).astype(ml_dtypes.bfloat16).astype(np.float64), axis, -1)
    blocks = v.reshape(v.shape[:-1] + (-1, 32))
    amax = np.abs(blocks).max(-1, keepdims=True)
    byte = np.maximum(np.where(amax > 0, np.frexp(amax)[1] - 1 + 127, 0) - down, 1)
    scale = np.exp2(byte - 127.0)
    codes = (blocks / scale).astype(np.float32).astype(dtype).astype(np.float64)
    return np.moveaxis((codes * scale).reshape(v.shape), -1, axis)


WIDE = False


def mx_kscale(k):
    if not WIDE:
        return np.ones(k)
    levels = np.array([10, -10, 5, -5, 0])
    if k % 512:
        return np.exp2(np.random.permutation(np.resize(levels, k // 32))).repeat(32)
    a = np.empty((k // 512, 16))
    for p in range(k // 512):
        a[p, :8] = np.random.permutation(np.resize(levels, 8))
        for g in range(8):
            far = levels[np.abs(levels - a[p, g]) >= 10]
            a[p, g + 8] = far[np.random.randint(len(far))]
    return np.exp2(a.ravel()).repeat(32)


def f64(x):
    return np.asarray(x).astype(np.float64)


def striped(idx):
    return np.tile(idx.reshape(-1, 16).T, (8, 1)).astype(np.uint16)


def unstriped(offs):
    return offs[:16].T.reshape(-1).astype(np.int64)


E2M1 = np.array([0.0, 0.5, 1.0, 1.5, 2.0, 3.0, 4.0, 6.0, -0.0, -0.5, -1.0, -1.5, -2.0, -3.0, -4.0, -6.0])


def pack_weight(w, fmt):
    k, n = w.shape
    w = f64(np.asarray(w, np.float32).astype(ml_dtypes.bfloat16)).reshape(k // 32, 32, n)
    amax = np.abs(w).max(1)
    if fmt == "e4m3":
        byte = np.frexp(amax)[1] - 1 + 127 - 7
    else:
        mant, ex = np.frexp(amax / 6.0)
        byte = np.where(mant > 0.5, ex, ex - 1) + 127
    byte = np.clip(np.where(amax > 0, byte, 1), 1, 254)
    scaled = (w * np.exp2(127.0 - byte)[:, None, :]).reshape(k, n).astype(np.float32)
    by_word = np.ascontiguousarray(scaled.reshape(k // 512, 128, 4, n).transpose(0, 1, 3, 2))
    if fmt == "e4m3":
        words = by_word.astype(ml_dtypes.float8_e4m3fn).view(np.uint8)
    else:
        c = by_word.astype(ml_dtypes.float4_e2m1fn).view(np.uint8) & 0xF
        words = (c[..., 0::2] | (c[..., 1::2] << 4)).reshape(k // 512, 128, 2 * n)
    return np.ascontiguousarray(words), np.ascontiguousarray(byte.astype(np.uint8).reshape(k // 512, 16, n))


def unpack_weight(words, scales, fmt):
    g, _, n = scales.shape
    words = np.ascontiguousarray(words).reshape(g, 128, n, -1)
    if fmt == "e4m3":
        vals = words.view(ml_dtypes.float8_e4m3fn).astype(np.float64)
    else:
        nib = np.empty((g, 128, n, 4), np.uint8)
        nib[..., 0::2] = words & 0xF
        nib[..., 1::2] = words >> 4
        vals = E2M1[nib]
    vals = vals * np.repeat(np.exp2(scales.astype(np.float64) - 127.0), 8, axis=1)[..., None]
    return vals.transpose(0, 1, 3, 2).reshape(g * 512, n)


def gelu(v):
    return 0.5 * v * (1.0 + np.tanh(np.sqrt(2.0 / np.pi) * (v + 0.044715 * v**3)))


def bf(x):
    return np.asarray(x, np.float32).astype(ml_dtypes.bfloat16)


def planes(Y):
    n, m = Y.shape
    b = f64(bf(Y)).reshape(n // 32, 32, m)
    amax = np.abs(b).max(1)
    byte = np.clip(np.where(amax > 0, np.frexp(amax)[1] - 1 + 127 - 7, 1), 1, 254)
    codes = (b * np.exp2(127.0 - byte)[:, None, :]).reshape(n, m).astype(np.float32).astype(ml_dtypes.float8_e4m3fn).view(np.uint8)
    words = codes.reshape(n // 512, 128, 4, m).transpose(0, 1, 3, 2)
    return np.ascontiguousarray(words), np.ascontiguousarray(byte.astype(np.uint8).reshape(n // 512, 16, m))


K, H, T, S, T2, P = 1024, 512, 2048, 1024, 2048, 1024

def setup_inputs():
    n = np.random.standard_normal
    s = mx_kscale(K)[:, None]
    u = mx_kscale(H)[:, None]
    d = {}
    d["tab_words"], d["tab_scales"] = pack_weight(n((K, T)) * s, "e4m3")
    d["wa"] = (n((K, H)) / K ** 0.5 / s * u.T).astype(np.float32)
    d["wb_words"], d["wb_scales"] = pack_weight(n((K, H)) / K ** 0.5 / s, "e2m1")
    d["wc_words"], d["wc_scales"] = pack_weight(0.9 * n((K, H)) / K ** 0.5 / s * u.T, "e4m3")
    d["wo"] = (1.4 * n((H, H)) / H ** 0.5 / u).astype(np.float32)
    d["page0"] = (1.2 * n((H, T2)) * u).astype(np.float32)
    d["wgs"] = np.exp(0.3 * n((128, S))).astype(np.float32)
    d["down"] = (np.exp(0.3 * n(H)) / u[:, 0]).astype(np.float32)
    d["gain"] = (np.exp(0.3 * n(H)) * u[:, 0]).astype(np.float32)
    d["adj"] = (np.exp(0.8 * n(H)) / u[:, 0]).astype(np.float32)
    d["offs"] = striped(np.random.permutation(T)[:S])
    d["offs2"] = striped(np.random.permutation(T2)[:S])
    d["offs3"] = striped(np.random.permutation(T2)[:P])
    d["offs4"] = striped(np.random.permutation(T2)[:P])
    return d

def reference(tab_words, tab_scales, wa, wb_words, wb_scales, wc_words, wc_scales, wo, page0, wgs, down, gain, adj, offs, offs2, offs3, offs4):
    v = unpack_weight(tab_words, tab_scales, "e4m3")[:, unstriped(offs)]
    a = mxq(f64(wa), 0, "e4m3").T @ v
    b = unpack_weight(wb_words, wb_scales, "e2m1").T @ v
    c = unpack_weight(wc_words, wc_scales, "e4m3").T @ v
    h = a * b + c
    page = f64(page0).copy()
    page[:, unstriped(offs2)] = np.tile(f64(wgs), (H // 128, 1)) * h
    x = page[:, unstriped(offs3)] * f64(down)[:, None]
    z = 0.5 * x * (1.0 + np.tanh(0.7978845608 * (x + 0.044715 * x ** 3))) * f64(gain)[:, None]
    f = mxq(f64(wo), 0, "e4m3").T @ mxq(z, 0, "e4m3")
    y = np.tanh(f) * (page[:, unstriped(offs4)] * f64(adj)[:, None])
    words, scales = planes(y)
    return y, words, scales

@@ -1,0 +1,285 @@
+from contextlib import ExitStack
+
+import concourse.mybir as mybir
+from concourse.masks import make_identity
+
+K, H, T, S, T2, NP = 1024, 512, 2048, 1024, 2048, 1024
+FLOPS = 2 * 3 * K * H * S + 2 * H * H * NP
+
+F32 = mybir.dt.float32
+BF16 = mybir.dt.bfloat16
+I32 = mybir.dt.int32
+U32 = mybir.dt.uint32
+U16 = mybir.dt.uint16
+U8 = mybir.dt.uint8
+FP8X4 = mybir.dt.float8_e4m3fn_x4
+FP4X4 = mybir.dt.float4_e2m1fn_x4
+MULT = mybir.AluOpType.mult
+ACT = mybir.ActivationFunctionType
+
+P = 128
+HALF = 512
+QUARTER = 256
+
+
+def cols(start, stop):
+    return slice(start // 16, stop // 16)
+
+
+def weave(copy, dst, src):
+    copy(out=dst.rearrange("p (c i) t -> p c t i", i=4), in_=src.rearrange("p t (c i) -> p c t i", i=4))
+
+
+def tile_list_gritting_surface_page_kernel(
+    tc, tab_words, tab_scales, wa, wb_words, wb_scales, wc_words, wc_scales, wo, page0, wgs,
+    down, gain, adj, offs, offs2, offs3, offs4, out_0, out_1, out_2,
+):
+    nc = tc.nc
+    with ExitStack() as ctx:
+        lists = ctx.enter_context(tc.tile_pool(name="lists", bufs=1))
+        keep = ctx.enter_context(tc.tile_pool(name="keep", bufs=1))
+        ring = ctx.enter_context(tc.tile_pool(name="ring", bufs=2))
+        psum = ctx.enter_context(tc.psum_pool(name="psum", bufs=2))
+
+        idx = lists.tile([P, S // 16], U16, name="idx")
+        idx2 = lists.tile([P, S // 16], U16, name="idx2")
+        idx3 = lists.tile([P, NP // 16], U16, name="idx3")
+        idx4 = lists.tile([P, NP // 16], U16, name="idx4")
+
+        tab_w = [keep.tile([P, T], U32, name="tab_w%d" % a, align_bytes=64) for a in range(2)]
+        tab_s = keep.tile([P, T], U8, name="tab_s", align_bytes=64)
+        w_s = keep.tile([P, 4 * H], U8, name="w_s", align_bytes=64)
+        v_s1 = [keep.tile([P, HALF], U8, name="v_s1_%d" % h, align_bytes=64) for h in range(2)]
+        nc.gpsimd.memset(tab_s[:].bitcast(I32), 0)
+        nc.vector.memset(w_s[:].bitcast(I32), 0)
+
+        nc.sync.dma_start(idx[:], offs)
+        for a in range(2):
+            nc.sync.dma_start(tab_w[a][:].bitcast(I32), tab_words[a].rearrange("p t i -> p (t i)").bitcast(I32))
+        for q in range(4):
+            nc.gpsimd.dma_start(tab_s[32 * q : 32 * q + 8, :].bitcast(I32), tab_scales[:, 4 * q : 4 * q + 4, :].bitcast(I32))
+        for n, scales in enumerate((wc_scales, wb_scales)):
+            for q in range(4):
+                nc.gpsimd.dma_start(
+                    w_s[32 * q : 32 * q + 4, 2 * H * n : 2 * H * (n + 1)].bitcast(I32).rearrange("r (a c) -> r a c", a=2),
+                    scales[:, 4 * q : 4 * q + 4, :].bitcast(I32).rearrange("a r c -> r a c"),
+                )
+        for h in range(2):
+            nc.vector.memset(v_s1[h][:].bitcast(I32), 0)
+        ident = keep.tile([P, P], F32, name="ident")
+        make_identity(nc, ident[:])
+
+        wa_raw = [keep.tile([P, 4, H], F32, name="wa_raw%d" % a) for a in range(2)]
+        for a in range(2):
+            nc.sync.dma_start(wa_raw[a][:], wa[512 * a : 512 * (a + 1), :].rearrange("(p i) c -> p i c", i=4))
+        wb_w = keep.tile([P, 2, 2 * H], U8, name="wb_w", align_bytes=64)
+        nc.sync.dma_start(wb_w[:].bitcast(I32), wb_words.bitcast(I32).rearrange("a p c -> p a c"))
+        wc_w = keep.tile([P, 2, H], U32, name="wc_w", align_bytes=64)
+        nc.sync.dma_start(wc_w[:].bitcast(I32), wc_words.rearrange("a p c i -> p a (c i)").bitcast(I32))
+        nc.sync.dma_start(idx2[:], offs2)
+
+        wgs_rows = wgs.rearrange("(m t) j -> m t j", t=4)
+        wgs_a = keep.tile([P, 2, QUARTER], F32, name="wgs_a")
+        wgs_b = keep.tile([P, 2, S - QUARTER], F32, name="wgs_b")
+        wgs_c = keep.tile([P, 2, S], F32, name="wgs_c")
+        page = [keep.tile([P, T2], F32, name="page%d" % t) for t in range(4)]
+        page_rows = page0.rearrange("(p t) c -> p t c", t=4)
+
+        def load_wgs(tile, src):
+            for q in (0, 2, 1, 3):
+                nc.sync.dma_start(tile[32 * q : 32 * q + 32], src)
+
+        load_wgs(wgs_a, wgs_rows[:, 0:2, 0:QUARTER])
+        nc.sync.dma_start(page[0][:], page_rows[:, 0, :])
+        nc.sync.dma_start(page[1][:], page_rows[:, 1, :])
+        load_wgs(wgs_b, wgs_rows[:, 0:2, QUARTER:S])
+        nc.sync.dma_start(page[2][:], page_rows[:, 2, :])
+        load_wgs(wgs_c, wgs_rows[:, 2:4, :])
+        nc.sync.dma_start(idx3[:], offs3)
+        vec = {}
+        for name, src in (("down", down), ("gain", gain), ("adj", adj)):
+            vec[name] = keep.tile([P, 4], F32, name=name)
+            nc.sync.dma_start(vec[name][:], src.rearrange("(p t) -> p t", t=4))
+        wo_raw = keep.tile([P, 4, H], F32, name="wo_raw")
+        nc.sync.dma_start(wo_raw[:], wo.rearrange("(p i) c -> p i c", i=4))
+        nc.sync.dma_start(page[3][:], page_rows[:, 3, :])
+        nc.sync.dma_start(idx4[:], offs4)
+
+        def wgs_of(t, start, stop):
+            if t >= 2:
+                return wgs_c[:, t - 2, start:stop]
+            if stop <= QUARTER:
+                return wgs_a[:, t, start:stop]
+            return wgs_b[:, t, start - QUARTER : stop - QUARTER]
+
+        v_w = [[keep.tile([P, HALF], U32, name="v_w%d%d" % (a, h), align_bytes=64) for h in range(2)] for a in range(2)]
+        v_s = [keep.tile([P, HALF], U8, name="v_s%d" % h, align_bytes=64) for h in range(2)]
+
+        def gather_words(a, h):
+            nc.vector.tensor_copy(v_w[a][h][:], tab_w[a][:].indirect(idx[:, cols(HALF * h, HALF * (h + 1))]))
+
+        def gather_scales(h):
+            nc.vector.tensor_copy(v_s[h][:], tab_s[:].indirect(idx[:, cols(HALF * h, HALF * (h + 1))]))
+            nc.gpsimd.dma_start(v_s1[h][0:112, :].bitcast(I32), v_s[h][4:116, :].bitcast(I32))
+
+        wa_w = keep.tile([P, 2, H], U32, name="wa_w", align_bytes=64)
+        wa_s = keep.tile([P, 2, H], U8, name="wa_s", align_bytes=64)
+
+        def quantize_wa(a, shares):
+            for n, (copy, c0, c1) in enumerate(shares):
+                bf = keep.tile([P, c1 - c0, 4], BF16, name="wa_bf%d%d" % (a, n), align_bytes=64)
+                weave(copy, bf[:], wa_raw[a][:, :, c0:c1])
+                nc.vector.quantize_mx(
+                    out=wa_w[:, a, c0:c1].bitcast(FP8X4), scales=wa_s[:, a, c0:c1], in_=bf[:].rearrange("p c i -> p (c i)")
+                )
+
+        gather_words(0, 0)
+        gather_words(1, 0)
+        gather_scales(0)
+        gather_words(0, 1)
+        quantize_wa(0, [(nc.scalar.copy, 0, H)])
+        gather_words(1, 1)
+        quantize_wa(1, [(nc.vector.tensor_copy, 0, H // 2), (nc.scalar.copy, H // 2, H)])
+        gather_scales(1)
+
+        h_all = keep.tile([P, 4, S], F32, name="h_all", tag="h_then_adjoining")
+
+        def first_stage(b):
+            h, c0 = divmod(P * b, HALF)
+            entries = slice(c0, c0 + P)
+            sums = {}
+            for name in ("a", "c", "b"):
+                acc = psum.tile([P, H], F32, name="acc_" + name, tag="acc_" + name)
+                for a in range(2):
+                    if name == "a":
+                        rhs, rhs_scale = wa_w[:, a, :].bitcast(FP8X4), wa_s[:, a, :]
+                    elif name == "c":
+                        rhs, rhs_scale = wc_w[:, a, :].bitcast(FP8X4), w_s[:, H * a : H * (a + 1)]
+                    else:
+                        rhs, rhs_scale = wb_w[:, a, :].bitcast(FP4X4), w_s[:, H * (2 + a) : H * (3 + a)]
+                    if a == 0:
+                        v_scale = v_s[h][:, entries]
+                    elif name == "b":
+                        v_scale = v_s1[h][:, entries]
+                    else:
+                        v_scale = v_s[h][4:P, entries]
+                    nc.tensor.matmul_mx(
+                        out=acc[:], lhsT=v_w[a][h][:, entries].bitcast(FP8X4), lhsT_scale=v_scale,
+                        rhs=rhs, rhs_scale=rhs_scale, start=(a == 0), stop=(a == 1),
+                    )
+                sums[name] = acc[:].rearrange("j (m t) -> j t m", t=4)
+            a_sb = ring.tile([P, 4, P], F32, name="a_sb")
+            c_sb = ring.tile([P, 4, P], F32, name="c_sb")
+            ab_sb = ring.tile([P, 4, P], F32, name="ab_sb")
+            nc.scalar.copy(out=a_sb[:], in_=sums["a"])
+            nc.scalar.copy(out=c_sb[:], in_=sums["c"])
+            nc.vector.tensor_tensor(ab_sb[:], sums["b"], a_sb[:], MULT)
+            return c_sb, ab_sb
+
+        def turn(b, c_sb, ab_sb):
+            turned = psum.tile([P, 4, P], F32, name="turned")
+            for t in range(4):
+                nc.tensor.matmul(turned[:, t, :], lhsT=c_sb[:, t, :], rhs=ident[:], is_transpose=True, start=True, stop=False)
+                nc.tensor.matmul(turned[:, t, :], lhsT=ab_sb[:, t, :], rhs=ident[:], is_transpose=True, start=False, stop=True)
+            nc.scalar.copy(out=h_all[:, :, P * b : P * (b + 1)], in_=turned[:])
+
+        def scatter(t, start, stop):
+            nc.vector.tensor_tensor(
+                page[t][:].indirect(idx2[:, cols(start, stop)]), h_all[:, t, start:stop], wgs_of(t, start, stop), MULT
+            )
+
+        z_bf = [keep.tile([P, HALF, 4], BF16, name="z_bf%d" % h, align_bytes=64) for h in range(2)]
+
+        def make_z(t):
+            for h in range(2):
+                x = ring.tile([P, HALF], F32, name="x")
+                nc.vector.tensor_copy(x[:], page[t][:].indirect(idx3[:, cols(HALF * h, HALF * (h + 1))]))
+                g = ring.tile([P, HALF], F32, name="g")
+                nc.scalar.activation(g[:], x[:], ACT.Gelu_apprx_tanh, scale=vec["down"][:, t : t + 1])
+                nc.scalar.activation(z_bf[h][:, :, t], g[:], ACT.Copy, scale=vec["gain"][:, t : t + 1])
+
+        wo_w = keep.tile([P, H], U32, name="wo_w", align_bytes=64)
+        wo_s = keep.tile([P, H], U8, name="wo_s", align_bytes=64)
+
+        def quantize_wo():
+            bf = keep.tile([P, H, 4], BF16, name="wo_bf", align_bytes=64)
+            nc.scalar.copy(
+                out=bf[:].rearrange("p (t m) i -> p m i t", t=4), in_=wo_raw[:].rearrange("p i (m t) -> p m i t", t=4)
+            )
+            nc.vector.quantize_mx(out=wo_w[:].bitcast(FP8X4), scales=wo_s[:], in_=bf[:].rearrange("p c i -> p (c i)"))
+
+        after_block = {
+            1: [(0, 0, 256), (1, 0, 256)],
+            3: [(0, 256, 512), (1, 256, 512)],
+            5: [(0, 512, 768), (1, 512, 768), (2, 0, 512)],
+        }
+        pending = first_stage(0)
+        for b in range(8):
+            ahead = first_stage(b + 1) if b < 7 else None
+            turn(b, *pending)
+            pending = ahead
+            for piece in after_block.get(b, []):
+                scatter(*piece)
+        quantize_wo()
+        scatter(0, 768, 1024)
+        make_z(0)
+        scatter(1, 768, 1024)
+        make_z(1)
+        scatter(2, 512, 1024)
+        make_z(2)
+        scatter(3, 0, 1024)
+        make_z(3)
+
+        adjoining = keep.tile([P, 4, NP], F32, name="adjoining", tag="h_then_adjoining")
+        y = [keep.tile([P, 4, HALF], F32, name="y%d" % h) for h in range(2)]
+        y_w = keep.tile([P, NP], U32, name="y_w", align_bytes=64)
+        y_s = keep.tile([P, NP], U8, name="y_s", align_bytes=64)
+        out_rows = out_0.rearrange("(p t) j -> p t j", t=4)
+        out_words = out_1[0].rearrange("p m t -> p (m t)").bitcast(I32)
+        banks = ("acc_a", "acc_c", "acc_b")
+
+        def second_stage(h):
+            z_w = keep.tile([P, HALF], U32, name="z_w%d" % h, align_bytes=64)
+            z_s = keep.tile([P, HALF], U8, name="z_s%d" % h, align_bytes=64)
+            nc.vector.quantize_mx(out=z_w[:].bitcast(FP8X4), scales=z_s[:], in_=z_bf[h][:].rearrange("p c i -> p (c i)"))
+            for t in range(4):
+                f = psum.tile([P, HALF], F32, name="f", tag=banks[(4 * h + t) % 3])
+                nc.tensor.matmul_mx(
+                    out=f[:], lhsT=wo_w[:, P * t : P * (t + 1)].bitcast(FP8X4), lhsT_scale=wo_s[:, P * t : P * (t + 1)],
+                    rhs=z_w[:].bitcast(FP8X4), rhs_scale=z_s[:], start=True, stop=True,
+                )
+                nc.scalar.activation(y[h][:, t, :], f[:], ACT.Tanh)
+
+        def gather_adjoining(t):
+            nc.vector.tensor_copy(adjoining[:, t, :], page[t][:].indirect(idx4[:]))
+
+        def finish(h, c0, c1, copy, y_bf):
+            for t in range(4):
+                nc.vector.scalar_tensor_tensor(
+                    y[h][:, t, c0:c1], adjoining[:, t, HALF * h + c0 : HALF * h + c1], vec["adj"][:, t : t + 1],
+                    y[h][:, t, c0:c1], MULT, MULT,
+                )
+            nc.sync.dma_start(out_rows[:, :, HALF * h + c0 : HALF * h + c1], y[h][:, :, c0:c1])
+            weave(copy, y_bf[:, c0:c1, :], y[h][:, :, c0:c1])
+
+        def planes(h, y_bf):
+            span = slice(HALF * h, HALF * (h + 1))
+            nc.vector.quantize_mx(out=y_w[:, span].bitcast(FP8X4), scales=y_s[:, span], in_=y_bf[:].rearrange("p c i -> p (c i)"))
+            nc.sync.dma_start(out_words[:, span], y_w[:, span].bitcast(I32))
+
+        gather_adjoining(0)
+        second_stage(0)
+        gather_adjoining(1)
+        second_stage(1)
+        gather_adjoining(2)
+        gather_adjoining(3)
+        y_bf0 = keep.tile([P, HALF, 4], BF16, name="y_bf0", align_bytes=64)
+        finish(0, 0, HALF, nc.scalar.copy, y_bf0)
+        y_bf1 = keep.tile([P, HALF, 4], BF16, name="y_bf1", align_bytes=64)
+        finish(1, 0, QUARTER, nc.scalar.copy, y_bf1)
+        planes(0, y_bf0)
+        finish(1, QUARTER, HALF, nc.vector.tensor_copy, y_bf1)
+        planes(1, y_bf1)
+        for q in range(4):
+            eng = nc.scalar if q % 2 else nc.sync
+            eng.dma_start(out_2[0, 4 * q : 4 * q + 4, :].bitcast(I32), y_s[32 * q : 32 * q + 4, :].bitcast(I32))

@@ -47,41 +47,48 @@ def tile_list_gritting_surface_page_kernel(
         idx4 = lists.tile([P, NP // 16], U16, name="idx4")
 
         tab_w = [keep.tile([P, T], U32, name="tab_w%d" % a, align_bytes=64) for a in range(2)]
-        tab_s = keep.tile([P, T], U8, name="tab_s", align_bytes=64)
-        w_s = keep.tile([P, 4 * H], U8, name="w_s", align_bytes=64)
-        v_s1 = [keep.tile([P, HALF], U8, name="v_s1_%d" % h, align_bytes=64) for h in range(2)]
-        nc.gpsimd.memset(tab_s[:].bitcast(I32), 0)
-        nc.vector.memset(w_s[:].bitcast(I32), 0)
+        tab_s = keep.tile([P, 2 * T], U8, name="tab_s", align_bytes=64)
+        wb_s = keep.tile([P, 2 * H], U8, name="wb_s", align_bytes=64)
+        wc_s = keep.tile([P, 2 * H], U8, name="wc_s", align_bytes=64)
+        nc.gpsimd.memset(tab_s[:, 0:T].bitcast(I32), 0)
+        nc.vector.memset(tab_s[:, T : 2 * T].bitcast(I32), 0)
+        nc.gpsimd.memset(wc_s[:].bitcast(I32), 0)
+        nc.gpsimd.memset(wb_s[:].bitcast(I32), 0)
 
-        nc.sync.dma_start(idx[:], offs)
-        for a in range(2):
+        def load_table(a):
             nc.sync.dma_start(tab_w[a][:].bitcast(I32), tab_words[a].rearrange("p t i -> p (t i)").bitcast(I32))
+
+        def load_scales(tile, scales, q):
+            nc.sync.dma_start(
+                tile[32 * q : 32 * q + 4, :].bitcast(I32).rearrange("r (a c) -> r a c", a=2),
+                scales[:, 4 * q : 4 * q + 4, :].bitcast(I32).rearrange("a r c -> r a c"),
+            )
+
+        wb_w = keep.tile([P, 2, 2 * H], U8, name="wb_w", align_bytes=64)
+        wc_w = keep.tile([P, 2, H], U32, name="wc_w", align_bytes=64)
+        wa_raw = [keep.tile([P, 4, H], F32, name="wa_raw%d" % a) for a in range(2)]
+        nc.sync.dma_start(idx[:], offs)
+        load_table(0)
         for q in range(4):
-            nc.gpsimd.dma_start(tab_s[32 * q : 32 * q + 8, :].bitcast(I32), tab_scales[:, 4 * q : 4 * q + 4, :].bitcast(I32))
-        for n, scales in enumerate((wc_scales, wb_scales)):
-            for q in range(4):
-                nc.gpsimd.dma_start(
-                    w_s[32 * q : 32 * q + 4, 2 * H * n : 2 * H * (n + 1)].bitcast(I32).rearrange("r (a c) -> r a c", a=2),
-                    scales[:, 4 * q : 4 * q + 4, :].bitcast(I32).rearrange("a r c -> r a c"),
-                )
-        for h in range(2):
-            nc.vector.memset(v_s1[h][:].bitcast(I32), 0)
+            load_scales(tab_s, tab_scales, q)
+        load_table(1)
+        load_scales(wc_s, wc_scales, 0)
+        load_scales(wc_s, wc_scales, 1)
+        nc.sync.dma_start(wc_w[:].bitcast(I32), wc_words.rearrange("a p c i -> p a (c i)").bitcast(I32))
+        load_scales(wc_s, wc_scales, 2)
+        load_scales(wc_s, wc_scales, 3)
+        nc.sync.dma_start(wb_w[:].bitcast(I32), wb_words.bitcast(I32).rearrange("a p c -> p a c"))
+        nc.sync.dma_start(wa_raw[0][:], wa[0:512, :].rearrange("(p i) c -> p i c", i=4))
+        for q in range(4):
+            load_scales(wb_s, wb_scales, q)
+        nc.sync.dma_start(wa_raw[1][:], wa[512:1024, :].rearrange("(p i) c -> p i c", i=4))
+        nc.sync.dma_start(idx2[:], offs2)
         ident = keep.tile([P, P], F32, name="ident")
         make_identity(nc, ident[:])
 
-        wa_raw = [keep.tile([P, 4, H], F32, name="wa_raw%d" % a) for a in range(2)]
-        for a in range(2):
-            nc.sync.dma_start(wa_raw[a][:], wa[512 * a : 512 * (a + 1), :].rearrange("(p i) c -> p i c", i=4))
-        wb_w = keep.tile([P, 2, 2 * H], U8, name="wb_w", align_bytes=64)
-        nc.sync.dma_start(wb_w[:].bitcast(I32), wb_words.bitcast(I32).rearrange("a p c -> p a c"))
-        wc_w = keep.tile([P, 2, H], U32, name="wc_w", align_bytes=64)
-        nc.sync.dma_start(wc_w[:].bitcast(I32), wc_words.rearrange("a p c i -> p a (c i)").bitcast(I32))
-        nc.sync.dma_start(idx2[:], offs2)
-
         wgs_rows = wgs.rearrange("(m t) j -> m t j", t=4)
-        wgs_a = keep.tile([P, 2, QUARTER], F32, name="wgs_a")
-        wgs_b = keep.tile([P, 2, S - QUARTER], F32, name="wgs_b")
-        wgs_c = keep.tile([P, 2, S], F32, name="wgs_c")
+        wgs_q = [keep.tile([P, 3, QUARTER], F32, name="wgs_q%d" % q) for q in range(4)]
+        wgs_3 = keep.tile([P, S], F32, name="wgs_3", tag="wgs_3", align_bytes=64)
         page = [keep.tile([P, T2], F32, name="page%d" % t) for t in range(4)]
         page_rows = page0.rearrange("(p t) c -> p t c", t=4)
 
@@ -89,91 +96,82 @@ def tile_list_gritting_surface_page_kernel(
             for q in (0, 2, 1, 3):
                 nc.sync.dma_start(tile[32 * q : 32 * q + 32], src)
 
-        load_wgs(wgs_a, wgs_rows[:, 0:2, 0:QUARTER])
-        nc.sync.dma_start(page[0][:], page_rows[:, 0, :])
-        nc.sync.dma_start(page[1][:], page_rows[:, 1, :])
-        load_wgs(wgs_b, wgs_rows[:, 0:2, QUARTER:S])
-        nc.sync.dma_start(page[2][:], page_rows[:, 2, :])
-        load_wgs(wgs_c, wgs_rows[:, 2:4, :])
+        load_wgs(wgs_q[0], wgs_rows[:, 0:3, 0:QUARTER])
+        for t in range(3):
+            nc.sync.dma_start(page[t][:], page_rows[:, t, :])
+        wo_raw = keep.tile([P, 4, H], F32, name="wo_raw")
+        for q in range(1, 4):
+            load_wgs(wgs_q[q], wgs_rows[:, 0:3, QUARTER * q : QUARTER * (q + 1)])
+            if q == 1:
+                nc.sync.dma_start(wo_raw[:], wo.rearrange("(p i) c -> p i c", i=4))
         nc.sync.dma_start(idx3[:], offs3)
         vec = {}
         for name, src in (("down", down), ("gain", gain), ("adj", adj)):
             vec[name] = keep.tile([P, 4], F32, name=name)
             nc.sync.dma_start(vec[name][:], src.rearrange("(p t) -> p t", t=4))
-        wo_raw = keep.tile([P, 4, H], F32, name="wo_raw")
-        nc.sync.dma_start(wo_raw[:], wo.rearrange("(p i) c -> p i c", i=4))
         nc.sync.dma_start(page[3][:], page_rows[:, 3, :])
+        load_wgs(wgs_3, wgs_rows[:, 3, :])
         nc.sync.dma_start(idx4[:], offs4)
 
         def wgs_of(t, start, stop):
-            if t >= 2:
-                return wgs_c[:, t - 2, start:stop]
-            if stop <= QUARTER:
-                return wgs_a[:, t, start:stop]
-            return wgs_b[:, t, start - QUARTER : stop - QUARTER]
+            if t == 3:
+                return wgs_3[:, start:stop]
+            return wgs_q[start // QUARTER][:, t, :]
 
         v_w = [[keep.tile([P, HALF], U32, name="v_w%d%d" % (a, h), align_bytes=64) for h in range(2)] for a in range(2)]
-        v_s = [keep.tile([P, HALF], U8, name="v_s%d" % h, align_bytes=64) for h in range(2)]
+        v_s = {}
 
         def gather_words(a, h):
             nc.vector.tensor_copy(v_w[a][h][:], tab_w[a][:].indirect(idx[:, cols(HALF * h, HALF * (h + 1))]))
 
-        def gather_scales(h):
-            nc.vector.tensor_copy(v_s[h][:], tab_s[:].indirect(idx[:, cols(HALF * h, HALF * (h + 1))]))
-            nc.gpsimd.dma_start(v_s1[h][0:112, :].bitcast(I32), v_s[h][4:116, :].bitcast(I32))
+        def gather_scales(a, h, tag):
+            v_s[a, h] = keep.tile([P, HALF], U8, name="v_s%d%d" % (a, h), tag=tag, align_bytes=64)
+            nc.vector.tensor_copy(v_s[a, h][:], tab_s[:, T * a : T * (a + 1)].indirect(idx[:, cols(HALF * h, HALF * (h + 1))]))
 
         wa_w = keep.tile([P, 2, H], U32, name="wa_w", align_bytes=64)
         wa_s = keep.tile([P, 2, H], U8, name="wa_s", align_bytes=64)
 
-        def quantize_wa(a, shares):
-            for n, (copy, c0, c1) in enumerate(shares):
-                bf = keep.tile([P, c1 - c0, 4], BF16, name="wa_bf%d%d" % (a, n), align_bytes=64)
-                weave(copy, bf[:], wa_raw[a][:, :, c0:c1])
-                nc.vector.quantize_mx(
-                    out=wa_w[:, a, c0:c1].bitcast(FP8X4), scales=wa_s[:, a, c0:c1], in_=bf[:].rearrange("p c i -> p (c i)")
-                )
+        def quantize_wa(a):
+            bf = keep.tile([P, H, 4], BF16, name="wa_bf%d" % a, tag="wa_bf%d" % a, align_bytes=64)
+            weave(nc.vector.tensor_copy, bf[:], wa_raw[a][:])
+            nc.vector.quantize_mx(out=wa_w[:, a, :].bitcast(FP8X4), scales=wa_s[:, a, :], in_=bf[:].rearrange("p c i -> p (c i)"))
 
         gather_words(0, 0)
+        gather_scales(0, 0, "v_s00")
+        gather_scales(1, 0, "v_s10")
         gather_words(1, 0)
-        gather_scales(0)
         gather_words(0, 1)
-        quantize_wa(0, [(nc.scalar.copy, 0, H)])
         gather_words(1, 1)
-        quantize_wa(1, [(nc.vector.tensor_copy, 0, H // 2), (nc.scalar.copy, H // 2, H)])
-        gather_scales(1)
+        quantize_wa(0)
+        quantize_wa(1)
+        gather_scales(0, 1, "wa_bf1")
 
-        h_all = keep.tile([P, 4, S], F32, name="h_all", tag="h_then_adjoining")
+        h_all = keep.tile([P, 4, S], F32, name="h_all")
 
         def first_stage(b):
             h, c0 = divmod(P * b, HALF)
             entries = slice(c0, c0 + P)
             sums = {}
-            for name in ("a", "c", "b"):
+            for name in ("c", "b", "a"):
                 acc = psum.tile([P, H], F32, name="acc_" + name, tag="acc_" + name)
                 for a in range(2):
                     if name == "a":
                         rhs, rhs_scale = wa_w[:, a, :].bitcast(FP8X4), wa_s[:, a, :]
                     elif name == "c":
-                        rhs, rhs_scale = wc_w[:, a, :].bitcast(FP8X4), w_s[:, H * a : H * (a + 1)]
+                        rhs, rhs_scale = wc_w[:, a, :].bitcast(FP8X4), wc_s[:, H * a : H * (a + 1)]
                     else:
-                        rhs, rhs_scale = wb_w[:, a, :].bitcast(FP4X4), w_s[:, H * (2 + a) : H * (3 + a)]
-                    if a == 0:
-                        v_scale = v_s[h][:, entries]
-                    elif name == "b":
-                        v_scale = v_s1[h][:, entries]
-                    else:
-                        v_scale = v_s[h][4:P, entries]
+                        rhs, rhs_scale = wb_w[:, a, :].bitcast(FP4X4), wb_s[:, H * a : H * (a + 1)]
                     nc.tensor.matmul_mx(
-                        out=acc[:], lhsT=v_w[a][h][:, entries].bitcast(FP8X4), lhsT_scale=v_scale,
+                        out=acc[:], lhsT=v_w[a][h][:, entries].bitcast(FP8X4), lhsT_scale=v_s[a, h][:, entries],
                         rhs=rhs, rhs_scale=rhs_scale, start=(a == 0), stop=(a == 1),
                     )
                 sums[name] = acc[:].rearrange("j (m t) -> j t m", t=4)
-            a_sb = ring.tile([P, 4, P], F32, name="a_sb")
-            c_sb = ring.tile([P, 4, P], F32, name="c_sb")
-            ab_sb = ring.tile([P, 4, P], F32, name="ab_sb")
-            nc.scalar.copy(out=a_sb[:], in_=sums["a"])
+            b_sb = keep.tile([P, 4, P], F32, name="b_sb%d" % b, tag="b_sb%d" % (b % 4 if b != 5 else 4), align_bytes=64)
+            c_sb = ring.tile([P, 4, P], F32, name="c_sb", bufs=4)
+            ab_sb = ring.tile([P, 4, P], F32, name="ab_sb", bufs=4)
             nc.scalar.copy(out=c_sb[:], in_=sums["c"])
-            nc.vector.tensor_tensor(ab_sb[:], sums["b"], a_sb[:], MULT)
+            nc.scalar.copy(out=b_sb[:], in_=sums["b"])
+            nc.vector.tensor_tensor(ab_sb[:], sums["a"], b_sb[:], MULT)
             return c_sb, ab_sb
 
         def turn(b, c_sb, ab_sb):
@@ -188,11 +186,11 @@ def tile_list_gritting_surface_page_kernel(
                 page[t][:].indirect(idx2[:, cols(start, stop)]), h_all[:, t, start:stop], wgs_of(t, start, stop), MULT
             )
 
-        z_bf = [keep.tile([P, HALF, 4], BF16, name="z_bf%d" % h, align_bytes=64) for h in range(2)]
+        z_bf = [keep.tile([P, HALF, 4], BF16, name="z_bf%d" % h, tag="z_bf%d" % h, align_bytes=64) for h in range(2)]
 
         def make_z(t):
             for h in range(2):
-                x = ring.tile([P, HALF], F32, name="x")
+                x = ring.tile([P, HALF], F32, name="x", bufs=6)
                 nc.vector.tensor_copy(x[:], page[t][:].indirect(idx3[:, cols(HALF * h, HALF * (h + 1))]))
                 g = ring.tile([P, HALF], F32, name="g")
                 nc.scalar.activation(g[:], x[:], ACT.Gelu_apprx_tanh, scale=vec["down"][:, t : t + 1])
@@ -202,35 +200,28 @@ def tile_list_gritting_surface_page_kernel(
         wo_s = keep.tile([P, H], U8, name="wo_s", align_bytes=64)
 
         def quantize_wo():
-            bf = keep.tile([P, H, 4], BF16, name="wo_bf", align_bytes=64)
+            bf = keep.tile([P, H, 4], BF16, name="wo_bf", tag="b_sb3", align_bytes=64)
             nc.scalar.copy(
                 out=bf[:].rearrange("p (t m) i -> p m i t", t=4), in_=wo_raw[:].rearrange("p i (m t) -> p m i t", t=4)
             )
             nc.vector.quantize_mx(out=wo_w[:].bitcast(FP8X4), scales=wo_s[:], in_=bf[:].rearrange("p c i -> p (c i)"))
 
-        after_block = {
-            1: [(0, 0, 256), (1, 0, 256)],
-            3: [(0, 256, 512), (1, 256, 512)],
-            5: [(0, 512, 768), (1, 512, 768), (2, 0, 512)],
-        }
-        pending = first_stage(0)
-        for b in range(8):
-            ahead = first_stage(b + 1) if b < 7 else None
-            turn(b, *pending)
-            pending = ahead
-            for piece in after_block.get(b, []):
-                scatter(*piece)
-        quantize_wo()
-        scatter(0, 768, 1024)
-        make_z(0)
-        scatter(1, 768, 1024)
-        make_z(1)
-        scatter(2, 512, 1024)
-        make_z(2)
-        scatter(3, 0, 1024)
+        made = [first_stage(b) for b in range(4)]
+        gather_scales(1, 1, "b_sb1")
+        for q in range(4):
+            turn(2 * q, *made[2 * q])
+            turn(2 * q + 1, *made[2 * q + 1])
+            if q < 2:
+                made.extend([first_stage(2 * q + 4), first_stage(2 * q + 5)])
+            for t in range(3):
+                scatter(t, QUARTER * q, QUARTER * (q + 1))
+                if q == 3:
+                    make_z(t)
+            if q == 2:
+                quantize_wo()
+        scatter(3, 0, S)
         make_z(3)
 
-        adjoining = keep.tile([P, 4, NP], F32, name="adjoining", tag="h_then_adjoining")
         y = [keep.tile([P, 4, HALF], F32, name="y%d" % h) for h in range(2)]
         y_w = keep.tile([P, NP], U32, name="y_w", align_bytes=64)
         y_s = keep.tile([P, NP], U8, name="y_s", align_bytes=64)
@@ -250,13 +241,19 @@ def tile_list_gritting_surface_page_kernel(
                 )
                 nc.scalar.activation(y[h][:, t, :], f[:], ACT.Tanh)
 
-        def gather_adjoining(t):
-            nc.vector.tensor_copy(adjoining[:, t, :], page[t][:].indirect(idx4[:]))
+        adjoining = {}
+
+        def gather_adjoining(h, pair, tag, align):
+            tile = keep.tile([P, 2, HALF], F32, name="adjoining%d%d" % (h, pair), tag=tag, align_bytes=align)
+            for n in range(2):
+                t = 2 * pair + n
+                nc.vector.tensor_copy(tile[:, n, :], page[t][:].indirect(idx4[:, cols(HALF * h, HALF * (h + 1))]))
+                adjoining[h, t] = tile[:, n, :]
 
         def finish(h, c0, c1, copy, y_bf):
             for t in range(4):
                 nc.vector.scalar_tensor_tensor(
-                    y[h][:, t, c0:c1], adjoining[:, t, HALF * h + c0 : HALF * h + c1], vec["adj"][:, t : t + 1],
+                    y[h][:, t, c0:c1], adjoining[h, t][:, c0:c1], vec["adj"][:, t : t + 1],
                     y[h][:, t, c0:c1], MULT, MULT,
                 )
             nc.sync.dma_start(out_rows[:, :, HALF * h + c0 : HALF * h + c1], y[h][:, :, c0:c1])
@@ -267,14 +264,14 @@ def tile_list_gritting_surface_page_kernel(
             nc.vector.quantize_mx(out=y_w[:, span].bitcast(FP8X4), scales=y_s[:, span], in_=y_bf[:].rearrange("p c i -> p (c i)"))
             nc.sync.dma_start(out_words[:, span], y_w[:, span].bitcast(I32))
 
-        gather_adjoining(0)
+        gather_adjoining(0, 0, "wgs_3", 64)
         second_stage(0)
-        gather_adjoining(1)
+        gather_adjoining(0, 1, "z_bf0", 64)
         second_stage(1)
-        gather_adjoining(2)
-        gather_adjoining(3)
+        gather_adjoining(1, 0, "z_bf1", 64)
         y_bf0 = keep.tile([P, HALF, 4], BF16, name="y_bf0", align_bytes=64)
         finish(0, 0, HALF, nc.scalar.copy, y_bf0)
+        gather_adjoining(1, 1, "wgs_3", 64)
         y_bf1 = keep.tile([P, HALF, 4], BF16, name="y_bf1", align_bytes=64)
         finish(1, 0, QUARTER, nc.scalar.copy, y_bf1)
         planes(0, y_bf0)

from contextlib import ExitStack

import concourse.mybir as mybir
from concourse.masks import make_identity

K, H, T, S, T2, NP = 1024, 512, 2048, 1024, 2048, 1024
FLOPS = 2 * 3 * K * H * S + 2 * H * H * NP

F32 = mybir.dt.float32
BF16 = mybir.dt.bfloat16
I32 = mybir.dt.int32
U32 = mybir.dt.uint32
U16 = mybir.dt.uint16
U8 = mybir.dt.uint8
FP8X4 = mybir.dt.float8_e4m3fn_x4
FP4X4 = mybir.dt.float4_e2m1fn_x4
MULT = mybir.AluOpType.mult
ACT = mybir.ActivationFunctionType

P = 128
HALF = 512
QUARTER = 256


def cols(start, stop):
    return slice(start // 16, stop // 16)


def weave(copy, dst, src):
    copy(out=dst.rearrange("p (c i) t -> p c t i", i=4), in_=src.rearrange("p t (c i) -> p c t i", i=4))


def tile_list_gritting_surface_page_kernel(
    tc, tab_words, tab_scales, wa, wb_words, wb_scales, wc_words, wc_scales, wo, page0, wgs,
    down, gain, adj, offs, offs2, offs3, offs4, out_0, out_1, out_2,
):
    nc = tc.nc
    with ExitStack() as ctx:
        lists = ctx.enter_context(tc.tile_pool(name="lists", bufs=1))
        keep = ctx.enter_context(tc.tile_pool(name="keep", bufs=1))
        ring = ctx.enter_context(tc.tile_pool(name="ring", bufs=2))
        psum = ctx.enter_context(tc.psum_pool(name="psum", bufs=2))

        idx = lists.tile([P, S // 16], U16, name="idx")
        idx2 = lists.tile([P, S // 16], U16, name="idx2")
        idx3 = lists.tile([P, NP // 16], U16, name="idx3")
        idx4 = lists.tile([P, NP // 16], U16, name="idx4")

        tab_w = [keep.tile([P, T], U32, name="tab_w%d" % a, align_bytes=64) for a in range(2)]
        tab_s = keep.tile([P, 2 * T], U8, name="tab_s", align_bytes=64)
        wb_s = keep.tile([P, 2 * H], U8, name="wb_s", align_bytes=64)
        wc_s = keep.tile([P, 2 * H], U8, name="wc_s", align_bytes=64)
        nc.gpsimd.memset(tab_s[:, 0:T].bitcast(I32), 0)
        nc.vector.memset(tab_s[:, T : 2 * T].bitcast(I32), 0)
        nc.gpsimd.memset(wc_s[:].bitcast(I32), 0)
        nc.gpsimd.memset(wb_s[:].bitcast(I32), 0)

        def load_table(a):
            nc.sync.dma_start(tab_w[a][:].bitcast(I32), tab_words[a].rearrange("p t i -> p (t i)").bitcast(I32))

        def load_scales(tile, scales, q):
            nc.sync.dma_start(
                tile[32 * q : 32 * q + 4, :].bitcast(I32).rearrange("r (a c) -> r a c", a=2),
                scales[:, 4 * q : 4 * q + 4, :].bitcast(I32).rearrange("a r c -> r a c"),
            )

        wb_w = keep.tile([P, 2, 2 * H], U8, name="wb_w", align_bytes=64)
        wc_w = keep.tile([P, 2, H], U32, name="wc_w", align_bytes=64)
        wa_raw = [keep.tile([P, 4, H], F32, name="wa_raw%d" % a) for a in range(2)]
        nc.sync.dma_start(idx[:], offs)
        load_table(0)
        for q in range(4):
            load_scales(tab_s, tab_scales, q)
        load_table(1)
        load_scales(wc_s, wc_scales, 0)
        load_scales(wc_s, wc_scales, 1)
        nc.sync.dma_start(wc_w[:].bitcast(I32), wc_words.rearrange("a p c i -> p a (c i)").bitcast(I32))
        load_scales(wc_s, wc_scales, 2)
        load_scales(wc_s, wc_scales, 3)
        nc.sync.dma_start(wb_w[:].bitcast(I32), wb_words.bitcast(I32).rearrange("a p c -> p a c"))
        nc.sync.dma_start(wa_raw[0][:], wa[0:512, :].rearrange("(p i) c -> p i c", i=4))
        for q in range(4):
            load_scales(wb_s, wb_scales, q)
        nc.sync.dma_start(wa_raw[1][:], wa[512:1024, :].rearrange("(p i) c -> p i c", i=4))
        nc.sync.dma_start(idx2[:], offs2)
        ident = keep.tile([P, P], F32, name="ident")
        make_identity(nc, ident[:])

        wgs_rows = wgs.rearrange("(m t) j -> m t j", t=4)
        wgs_q = [keep.tile([P, 3, QUARTER], F32, name="wgs_q%d" % q) for q in range(4)]
        wgs_3 = keep.tile([P, S], F32, name="wgs_3", tag="wgs_3", align_bytes=64)
        page = [keep.tile([P, T2], F32, name="page%d" % t) for t in range(4)]
        page_rows = page0.rearrange("(p t) c -> p t c", t=4)

        def load_wgs(tile, src):
            for q in (0, 2, 1, 3):
                nc.sync.dma_start(tile[32 * q : 32 * q + 32], src)

        load_wgs(wgs_q[0], wgs_rows[:, 0:3, 0:QUARTER])
        for t in range(3):
            nc.sync.dma_start(page[t][:], page_rows[:, t, :])
        wo_raw = keep.tile([P, 4, H], F32, name="wo_raw")
        for q in range(1, 4):
            load_wgs(wgs_q[q], wgs_rows[:, 0:3, QUARTER * q : QUARTER * (q + 1)])
            if q == 1:
                nc.sync.dma_start(wo_raw[:], wo.rearrange("(p i) c -> p i c", i=4))
        nc.sync.dma_start(idx3[:], offs3)
        vec = {}
        for name, src in (("down", down), ("gain", gain), ("adj", adj)):
            vec[name] = keep.tile([P, 4], F32, name=name)
            nc.sync.dma_start(vec[name][:], src.rearrange("(p t) -> p t", t=4))
        nc.sync.dma_start(page[3][:], page_rows[:, 3, :])
        load_wgs(wgs_3, wgs_rows[:, 3, :])
        nc.sync.dma_start(idx4[:], offs4)

        def wgs_of(t, start, stop):
            if t == 3:
                return wgs_3[:, start:stop]
            return wgs_q[start // QUARTER][:, t, :]

        v_w = [[keep.tile([P, HALF], U32, name="v_w%d%d" % (a, h), align_bytes=64) for h in range(2)] for a in range(2)]
        v_s = {}

        def gather_words(a, h):
            nc.vector.tensor_copy(v_w[a][h][:], tab_w[a][:].indirect(idx[:, cols(HALF * h, HALF * (h + 1))]))

        def gather_scales(a, h, tag):
            v_s[a, h] = keep.tile([P, HALF], U8, name="v_s%d%d" % (a, h), tag=tag, align_bytes=64)
            nc.vector.tensor_copy(v_s[a, h][:], tab_s[:, T * a : T * (a + 1)].indirect(idx[:, cols(HALF * h, HALF * (h + 1))]))

        wa_w = keep.tile([P, 2, H], U32, name="wa_w", align_bytes=64)
        wa_s = keep.tile([P, 2, H], U8, name="wa_s", align_bytes=64)

        def quantize_wa(a):
            bf = keep.tile([P, H, 4], BF16, name="wa_bf%d" % a, tag="wa_bf%d" % a, align_bytes=64)
            weave(nc.vector.tensor_copy, bf[:], wa_raw[a][:])
            nc.vector.quantize_mx(out=wa_w[:, a, :].bitcast(FP8X4), scales=wa_s[:, a, :], in_=bf[:].rearrange("p c i -> p (c i)"))

        gather_words(0, 0)
        gather_scales(0, 0, "v_s00")
        gather_scales(1, 0, "v_s10")
        gather_words(1, 0)
        gather_words(0, 1)
        gather_words(1, 1)
        quantize_wa(0)
        quantize_wa(1)
        gather_scales(0, 1, "wa_bf1")

        h_all = keep.tile([P, 4, S], F32, name="h_all")

        def first_stage(b):
            h, c0 = divmod(P * b, HALF)
            entries = slice(c0, c0 + P)
            sums = {}
            for name in ("c", "b", "a"):
                acc = psum.tile([P, H], F32, name="acc_" + name, tag="acc_" + name)
                for a in range(2):
                    if name == "a":
                        rhs, rhs_scale = wa_w[:, a, :].bitcast(FP8X4), wa_s[:, a, :]
                    elif name == "c":
                        rhs, rhs_scale = wc_w[:, a, :].bitcast(FP8X4), wc_s[:, H * a : H * (a + 1)]
                    else:
                        rhs, rhs_scale = wb_w[:, a, :].bitcast(FP4X4), wb_s[:, H * a : H * (a + 1)]
                    nc.tensor.matmul_mx(
                        out=acc[:], lhsT=v_w[a][h][:, entries].bitcast(FP8X4), lhsT_scale=v_s[a, h][:, entries],
                        rhs=rhs, rhs_scale=rhs_scale, start=(a == 0), stop=(a == 1),
                    )
                sums[name] = acc[:].rearrange("j (m t) -> j t m", t=4)
            b_sb = keep.tile([P, 4, P], F32, name="b_sb%d" % b, tag="b_sb%d" % (b % 4 if b != 5 else 4), align_bytes=64)
            c_sb = ring.tile([P, 4, P], F32, name="c_sb", bufs=4)
            ab_sb = ring.tile([P, 4, P], F32, name="ab_sb", bufs=4)
            nc.scalar.copy(out=c_sb[:], in_=sums["c"])
            nc.scalar.copy(out=b_sb[:], in_=sums["b"])
            nc.vector.tensor_tensor(ab_sb[:], sums["a"], b_sb[:], MULT)
            return c_sb, ab_sb

        def turn(b, c_sb, ab_sb):
            turned = psum.tile([P, 4, P], F32, name="turned")
            for t in range(4):
                nc.tensor.matmul(turned[:, t, :], lhsT=c_sb[:, t, :], rhs=ident[:], is_transpose=True, start=True, stop=False)
                nc.tensor.matmul(turned[:, t, :], lhsT=ab_sb[:, t, :], rhs=ident[:], is_transpose=True, start=False, stop=True)
            nc.scalar.copy(out=h_all[:, :, P * b : P * (b + 1)], in_=turned[:])

        def scatter(t, start, stop):
            nc.vector.tensor_tensor(
                page[t][:].indirect(idx2[:, cols(start, stop)]), h_all[:, t, start:stop], wgs_of(t, start, stop), MULT
            )

        z_bf = [keep.tile([P, HALF, 4], BF16, name="z_bf%d" % h, tag="z_bf%d" % h, align_bytes=64) for h in range(2)]

        def make_z(t):
            for h in range(2):
                x = ring.tile([P, HALF], F32, name="x", bufs=6)
                nc.vector.tensor_copy(x[:], page[t][:].indirect(idx3[:, cols(HALF * h, HALF * (h + 1))]))
                g = ring.tile([P, HALF], F32, name="g")
                nc.scalar.activation(g[:], x[:], ACT.Gelu_apprx_tanh, scale=vec["down"][:, t : t + 1])
                nc.scalar.activation(z_bf[h][:, :, t], g[:], ACT.Copy, scale=vec["gain"][:, t : t + 1])

        wo_w = keep.tile([P, H], U32, name="wo_w", align_bytes=64)
        wo_s = keep.tile([P, H], U8, name="wo_s", align_bytes=64)

        def quantize_wo():
            bf = keep.tile([P, H, 4], BF16, name="wo_bf", tag="b_sb3", align_bytes=64)
            nc.scalar.copy(
                out=bf[:].rearrange("p (t m) i -> p m i t", t=4), in_=wo_raw[:].rearrange("p i (m t) -> p m i t", t=4)
            )
            nc.vector.quantize_mx(out=wo_w[:].bitcast(FP8X4), scales=wo_s[:], in_=bf[:].rearrange("p c i -> p (c i)"))

        made = [first_stage(b) for b in range(4)]
        gather_scales(1, 1, "b_sb1")
        for q in range(4):
            turn(2 * q, *made[2 * q])
            turn(2 * q + 1, *made[2 * q + 1])
            if q < 2:
                made.extend([first_stage(2 * q + 4), first_stage(2 * q + 5)])
            for t in range(3):
                scatter(t, QUARTER * q, QUARTER * (q + 1))
                if q == 3:
                    make_z(t)
            if q == 2:
                quantize_wo()
        scatter(3, 0, S)
        make_z(3)

        y = [keep.tile([P, 4, HALF], F32, name="y%d" % h) for h in range(2)]
        y_w = keep.tile([P, NP], U32, name="y_w", align_bytes=64)
        y_s = keep.tile([P, NP], U8, name="y_s", align_bytes=64)
        out_rows = out_0.rearrange("(p t) j -> p t j", t=4)
        out_words = out_1[0].rearrange("p m t -> p (m t)").bitcast(I32)
        banks = ("acc_a", "acc_c", "acc_b")

        def second_stage(h):
            z_w = keep.tile([P, HALF], U32, name="z_w%d" % h, align_bytes=64)
            z_s = keep.tile([P, HALF], U8, name="z_s%d" % h, align_bytes=64)
            nc.vector.quantize_mx(out=z_w[:].bitcast(FP8X4), scales=z_s[:], in_=z_bf[h][:].rearrange("p c i -> p (c i)"))
            for t in range(4):
                f = psum.tile([P, HALF], F32, name="f", tag=banks[(4 * h + t) % 3])
                nc.tensor.matmul_mx(
                    out=f[:], lhsT=wo_w[:, P * t : P * (t + 1)].bitcast(FP8X4), lhsT_scale=wo_s[:, P * t : P * (t + 1)],
                    rhs=z_w[:].bitcast(FP8X4), rhs_scale=z_s[:], start=True, stop=True,
                )
                nc.scalar.activation(y[h][:, t, :], f[:], ACT.Tanh)

        adjoining = {}

        def gather_adjoining(h, pair, tag, align):
            tile = keep.tile([P, 2, HALF], F32, name="adjoining%d%d" % (h, pair), tag=tag, align_bytes=align)
            for n in range(2):
                t = 2 * pair + n
                nc.vector.tensor_copy(tile[:, n, :], page[t][:].indirect(idx4[:, cols(HALF * h, HALF * (h + 1))]))
                adjoining[h, t] = tile[:, n, :]

        def finish(h, c0, c1, copy, y_bf):
            for t in range(4):
                nc.vector.scalar_tensor_tensor(
                    y[h][:, t, c0:c1], adjoining[h, t][:, c0:c1], vec["adj"][:, t : t + 1],
                    y[h][:, t, c0:c1], MULT, MULT,
                )
            nc.sync.dma_start(out_rows[:, :, HALF * h + c0 : HALF * h + c1], y[h][:, :, c0:c1])
            weave(copy, y_bf[:, c0:c1, :], y[h][:, :, c0:c1])

        def planes(h, y_bf):
            span = slice(HALF * h, HALF * (h + 1))
            nc.vector.quantize_mx(out=y_w[:, span].bitcast(FP8X4), scales=y_s[:, span], in_=y_bf[:].rearrange("p c i -> p (c i)"))
            nc.sync.dma_start(out_words[:, span], y_w[:, span].bitcast(I32))

        gather_adjoining(0, 0, "wgs_3", 64)
        second_stage(0)
        gather_adjoining(0, 1, "z_bf0", 64)
        second_stage(1)
        gather_adjoining(1, 0, "z_bf1", 64)
        y_bf0 = keep.tile([P, HALF, 4], BF16, name="y_bf0", align_bytes=64)
        finish(0, 0, HALF, nc.scalar.copy, y_bf0)
        gather_adjoining(1, 1, "wgs_3", 64)
        y_bf1 = keep.tile([P, HALF, 4], BF16, name="y_bf1", align_bytes=64)
        finish(1, 0, QUARTER, nc.scalar.copy, y_bf1)
        planes(0, y_bf0)
        finish(1, QUARTER, HALF, nc.vector.tensor_copy, y_bf1)
        planes(1, y_bf1)
        for q in range(4):
            eng = nc.scalar if q % 2 else nc.sync
            eng.dma_start(out_2[0, 4 * q : 4 * q + 4, :].bitcast(I32), y_s[32 * q : 32 * q + 4, :].bitcast(I32))
